import numpy as np
import ml_dtypes


def mxq(x, axis, fmt="e4m3"):
    dtype, down = {"e4m3": (ml_dtypes.float8_e4m3fn, 7), "e5m2": (ml_dtypes.float8_e5m2, 14)}[fmt]
    v = np.moveaxis(np.asarray(x, np.float32).astype(ml_dtypes.bfloat16).astype(np.float64), axis, -1)
    blocks = v.reshape(v.shape[:-1] + (-1, 32))
    amax = np.abs(blocks).max(-1, keepdims=True)
    byte = np.maximum(np.where(amax > 0, np.frexp(amax)[1] - 1 + 127, 0) - down, 1)
    scale = np.exp2(byte - 127.0)
    codes = (blocks / scale).astype(np.float32).astype(dtype).astype(np.float64)
    return np.moveaxis((codes * scale).reshape(v.shape), -1, axis)


WIDE = False


def mx_kscale(k):
    if not WIDE:
        return np.ones(k)
    levels = np.array([30, -30])
    if k % 512:
        return np.exp2(np.random.permutation(np.resize(levels, k // 32))).repeat(32)
    a = np.empty((k // 512, 16))
    for p in range(k // 512):
        a[p, :8] = np.random.permutation(np.resize(levels, 8))
        for g in range(8):
            far = levels[np.abs(levels - a[p, g]) >= 10]
            a[p, g + 8] = far[np.random.randint(len(far))]
    return np.exp2(a.ravel()).repeat(32)


def f64(x):
    return np.asarray(x).astype(np.float64)


def striped(idx):
    return np.tile(np.asarray(idx).reshape(-1, 16).T, (8, 1)).astype(np.uint16)


def unstriped(offs):
    return offs[:16].T.reshape(-1).astype(np.int64)


E2M1 = np.array([0.0, 0.5, 1.0, 1.5, 2.0, 3.0, 4.0, 6.0, -0.0, -0.5, -1.0, -1.5, -2.0, -3.0, -4.0, -6.0])


def pack_weight(w, fmt):
    k, n = w.shape
    w = f64(np.asarray(w, np.float32).astype(ml_dtypes.bfloat16)).reshape(k // 32, 32, n)
    amax = np.abs(w).max(1)
    if fmt in ("e4m3", "e5m2"):
        byte = np.frexp(amax)[1] - 1 + 127 - (7 if fmt == "e4m3" else 14)
    else:
        mant, ex = np.frexp(amax / 6.0)
        byte = np.where(mant > 0.5, ex, ex - 1) + 127
    byte = np.clip(np.where(amax > 0, byte, 1), 1, 254)
    scaled = (w * np.exp2(127.0 - byte)[:, None, :]).reshape(k, n).astype(np.float32)
    by_word = np.ascontiguousarray(scaled.reshape(k // 512, 128, 4, n).transpose(0, 1, 3, 2))
    if fmt in ("e4m3", "e5m2"):
        words = by_word.astype(ml_dtypes.float8_e4m3fn if fmt == "e4m3" else ml_dtypes.float8_e5m2).view(np.uint8)
    else:
        c = by_word.astype(ml_dtypes.float4_e2m1fn).view(np.uint8) & 0xF
        words = (c[..., 0::2] | (c[..., 1::2] << 4)).reshape(k // 512, 128, 2 * n)
    return np.ascontiguousarray(words), np.ascontiguousarray(byte.astype(np.uint8).reshape(k // 512, 16, n))


def unpack_weight(words, scales, fmt):
    g, _, n = scales.shape
    words = np.ascontiguousarray(words).reshape(g, 128, n, -1)
    if fmt in ("e4m3", "e5m2"):
        vals = words.view(ml_dtypes.float8_e4m3fn if fmt == "e4m3" else ml_dtypes.float8_e5m2).astype(np.float64)
    else:
        nib = np.empty((g, 128, n, 4), np.uint8)
        nib[..., 0::2] = words & 0xF
        nib[..., 1::2] = words >> 4
        vals = E2M1[nib]
    vals = vals * np.repeat(np.exp2(scales.astype(np.float64) - 127.0), 8, axis=1)[..., None]
    return vals.transpose(0, 1, 3, 2).reshape(g * 512, n)


K, T, J, R, C, I, O, N, S, E = 512, 1024, 256, 512, 512, 128, 128, 256, 1024, 1024


def setup_inputs():
    n = np.random.standard_normal
    idx = np.random.permutation(T)[:J]
    idx2 = np.random.permutation(J)[:I]
    idx3 = np.random.permutation(C)[:I]
    idx4 = np.random.permutation(C)[:O]
    idx5 = np.random.permutation(J)[:O]
    idx6 = np.random.permutation(S)[:N]
    idx7 = np.random.permutation(E)[:O]
    fk = mx_kscale(K)
    fr = mx_kscale(R)
    xtp = pack_weight(n((K, T)) / fk[:, None], "e5m2")
    wp = pack_weight(n((K, R)) * 1 / np.sqrt(K) * fk[:, None] * fr, "e2m1")
    w2p = pack_weight(n((K, R)) * 1 / np.sqrt(K) * fk[:, None], "e4m3")
    vsp = pack_weight(n((R, S)) * 1 / np.sqrt(R) / fr[:, None], "e2m1")
    return {
        "xt_words": xtp[0],
        "xt_scales": xtp[1],
        "w_words": wp[0],
        "w_scales": wp[1],
        "w2_words": w2p[0],
        "w2_scales": w2p[1],
        "vs_words": vsp[0],
        "vs_scales": vsp[1],
        "offs": striped(idx),
        "offs2": striped(idx2),
        "offs3": striped(idx3),
        "offs4": striped(idx4),
        "offs5": striped(idx5),
        "offs6": striped(idx6),
        "offs7": striped(idx7),
    }


def reference(xt_words, xt_scales, w_words, w_scales, w2_words, w2_scales, vs_words, vs_scales, offs, offs2, offs3, offs4, offs5, offs6, offs7):
    idx = unstriped(offs)
    idx2 = unstriped(offs2)
    idx3 = unstriped(offs3)
    idx4 = unstriped(offs4)
    idx5 = unstriped(offs5)
    idx6 = unstriped(offs6)
    idx7 = unstriped(offs7)
    xtu = unpack_weight(xt_words, xt_scales, "e5m2")
    wu = unpack_weight(w_words, w_scales, "e2m1")
    w2u = unpack_weight(w2_words, w2_scales, "e4m3")
    vsu = unpack_weight(vs_words, vs_scales, "e2m1")
    xtidxg = xtu[:, idx]
    a = wu.T @ xtidxg
    b = w2u.T @ xtidxg
    lb = b[:, 0:1]
    la = a[:, 0:1]
    h1 = a[:, idx2] * lb
    pw = np.zeros((R, C))
    pw[:, idx3] = h1
    hid = np.maximum(pw[:, idx4], b[:, idx5] * la)
    vsidx6g = vsu[:, idx6]
    hidq = mxq(hid, 0, "e4m3")
    p = vsidx6g.T @ hidq
    y = np.zeros((N, E))
    y[:, idx7] = p
    return y

@@ -1,0 +1,180 @@
+from contextlib import ExitStack
+
+import concourse.mybir as mybir
+
+K, T, J, R, C, I, O, N, S, E = 512, 1024, 256, 512, 512, 128, 128, 256, 1024, 1024
+FLOPS = 2 * (2 * K * R * J + R * N * O)
+
+F32 = mybir.dt.float32
+BF16 = mybir.dt.bfloat16
+I32 = mybir.dt.int32
+U32 = mybir.dt.uint32
+U16 = mybir.dt.uint16
+U8 = mybir.dt.uint8
+E4M3 = mybir.dt.float8_e4m3fn_x4
+E5M2 = mybir.dt.float8_e5m2_x4
+E2M1 = mybir.dt.float4_e2m1fn_x4
+COPY = mybir.ActivationFunctionType.Copy
+MAX = mybir.AluOpType.max
+
+P = 128
+PACK = 4
+QUADS = 4
+
+
+def tile_list_leadseats_twow_store_scattered_kernel(
+    tc, xt_words, xt_scales, w_words, w_scales, w2_words, w2_scales, vs_words, vs_scales,
+    offs, offs2, offs3, offs4, offs5, offs6, offs7, out,
+):
+    nc = tc.nc
+    with ExitStack() as ctx:
+        lists = ctx.enter_context(tc.tile_pool(name="lists", bufs=1))
+        sb = ctx.enter_context(tc.tile_pool(name="sb", bufs=1))
+        psum = ctx.enter_context(tc.psum_pool(name="psum", bufs=1))
+
+        def tile(name, shape, dtype, tag=""):
+            return sb.tile(shape, dtype, name=name, tag=tag or name, align_bytes=64)
+
+        def load_list(name, src):
+            held = lists.tile([P, src.shape[1]], U16, name=name)
+            nc.sync.dma_start(held[:], src)
+            return held
+
+        def zero_bytes(plane):
+            nc.vector.memset(plane[:].bitcast(I32), 0)
+
+        def load_scale_rows(plane, scales):
+            rows = scales[0].bitcast(I32)
+            for q in range(QUADS):
+                nc.sync.dma_start(plane[:].bitcast(I32)[32 * q : 32 * q + 4, :], rows[4 * q : 4 * q + 4, :])
+
+        def stage_scale_rows(name, scales, queue):
+            staged = tile(name, [4, QUADS, R // 4], I32)
+            queue.dma_start(staged[:], scales[0].bitcast(I32).rearrange("(q r) c -> r q c", r=4))
+            return staged
+
+        def deal_scale_rows(name, staged, plane):
+            for q in range(QUADS):
+                nc.vector.tensor_copy(plane[:].bitcast(I32)[32 * q : 32 * q + 4, :], staged[:, q, :])
+            dealt = tile(name, [P, PACK, P], U8)
+            nc.vector.tensor_copy(dealt[:].rearrange("p t m -> p m t"), plane[:].rearrange("p (m t) -> p m t", t=PACK))
+            return dealt
+
+        xs_plane = tile("xs_plane", [P, T], U8)
+        ws_plane = tile("ws_plane", [P, R], U8)
+        w2s_plane = tile("w2s_plane", [P, R], U8)
+        vs_plane = tile("vs_plane", [P, S], U8)
+        for plane in (xs_plane, w2s_plane, ws_plane, vs_plane):
+            zero_bytes(plane)
+
+        idx = load_list("idx", offs)
+        w2s_staged = stage_scale_rows("w2s_staged", w2_scales, nc.scalar)
+        w2w = tile("w2w", [P, R], I32)
+        nc.sync.dma_start(w2w[:], w2_words[0].rearrange("p c t -> p (c t)").bitcast(I32))
+        xw = tile("xw", [P, T], I32)
+        nc.scalar.dma_start(xw[:], xt_words[0].rearrange("p c t -> p (c t)").bitcast(I32))
+        load_scale_rows(xs_plane, xt_scales)
+        ws_staged = stage_scale_rows("ws_staged", w_scales, nc.sync)
+        ww = tile("ww", [P, R], U16)
+        nc.sync.dma_start(ww[:].bitcast(I32), w_words[0].bitcast(I32))
+        idx2 = load_list("idx2", offs2)
+        idx3 = load_list("idx3", offs3)
+        idx6 = load_list("idx6", offs6)
+        vw = tile("vw", [P, S], U16)
+        nc.sync.dma_start(vw[:].bitcast(I32), vs_words[0].bitcast(I32))
+        idx5 = load_list("idx5", offs5)
+        idx4 = load_list("idx4", offs4)
+        load_scale_rows(vs_plane, vs_scales)
+        idx7 = load_list("idx7", offs7)
+
+        boards = [tile(f"board{t}", [P, C], F32) for t in range(PACK)]
+        for board in boards:
+            nc.vector.memset(board[:], 0.0)
+
+        w2s_dealt = deal_scale_rows("w2s_dealt", w2s_staged, w2s_plane)
+        w2w_dealt = tile("w2w_dealt", [P, PACK, P], U32)
+        nc.scalar.copy(w2w_dealt[:].rearrange("p t m -> p m t"), w2w[:].bitcast(U32).rearrange("p (m t) -> p m t", t=PACK))
+        xs_picked = tile("xs_picked", [P, J], U8)
+        nc.vector.tensor_copy(xs_picked[:], xs_plane[:].indirect(idx[:]))
+        xw_picked = tile("xw_picked", [P, J], U32, tag="xs_plane")
+        nc.vector.tensor_copy(xw_picked[:], xw[:].bitcast(U32).indirect(idx[:]))
+        ws_dealt = deal_scale_rows("ws_dealt", ws_staged, ws_plane)
+        ww_dealt = tile("ww_dealt", [P, PACK, P], U16)
+        nc.vector.tensor_copy(ww_dealt[:].rearrange("p t m -> p m t"), ww[:].rearrange("p (m t) -> p m t", t=PACK))
+
+        a_bank, b_bank = [], []
+        for t in range(PACK):
+            b_bank.append(psum.tile([P, J], F32, name=f"b_bank{t}", tag=f"bank{t}"))
+            nc.tensor.matmul_mx(
+                b_bank[t][:], lhsT=w2w_dealt[:, t, :].bitcast(E4M3), lhsT_scale=w2s_dealt[:, t, :],
+                rhs=xw_picked[:].bitcast(E5M2), rhs_scale=xs_picked[:], start=True, stop=True,
+            )
+        for t in range(PACK):
+            a_bank.append(psum.tile([P, J], F32, name=f"a_bank{t}", tag=f"bank{PACK + t}"))
+            nc.tensor.matmul_mx(
+                a_bank[t][:], lhsT=ww_dealt[:, t, :].bitcast(E2M1), lhsT_scale=ws_dealt[:, t, :],
+                rhs=xw_picked[:].bitcast(E5M2), rhs_scale=xs_picked[:], start=True, stop=True,
+            )
+
+        pages = [tile(f"page{h}", [P, E], F32, tag=tag) for h, tag in enumerate(("w2w_dealt", "ww_dealt"))]
+        for page in pages:
+            nc.gpsimd.memset(page[:], 0.0)
+
+        a = [tile(f"a{t}", [P, J], F32) for t in range(PACK)]
+        b = [tile(f"b{t}", [P, J], F32) for t in range(PACK)]
+        seats = [tile(f"seats{t}", [P, I], F32) for t in range(PACK)]
+        from_board = tile("from_board", [P, PACK, O], F32)
+        from_b = tile("from_b", [P, PACK, O], F32)
+
+        def seat(t):
+            nc.scalar.activation(seats[t][:], a[t][:].indirect(idx2[:]), COPY, scale=b[t][:, 0:1])
+
+        def rival(t):
+            nc.scalar.activation(from_b[:, t, :], b[t][:].indirect(idx5[:]), COPY, scale=a[t][:, 0:1])
+
+        for t in range(PACK):
+            nc.scalar.copy(b[t][:], b_bank[t][:])
+        for t in range(PACK):
+            nc.vector.tensor_copy(a[t][:], a_bank[t][:])
+            seat(t)
+        for t in (0, 1):
+            nc.vector.tensor_copy(boards[t][:].indirect(idx3[:]), seats[t][:])
+        for t in (2, 3):
+            nc.scalar.activation(boards[t][:].indirect(idx3[:]), seats[t][:], COPY)
+        vw_picked = tile("vw_picked", [P, N], U16)
+        nc.vector.tensor_copy(vw_picked[:], vw[:].indirect(idx6[:]))
+        for t in range(PACK):
+            rival(t)
+        for t in (0, 1, 2):
+            nc.vector.tensor_copy(from_board[:, t, :], boards[t][:].indirect(idx4[:]))
+        nc.scalar.activation(from_board[:, 3, :], boards[3][:].indirect(idx4[:]), COPY)
+        vs_picked = tile("vs_picked", [P, N], U8)
+        nc.vector.tensor_copy(vs_picked[:], vs_plane[:].indirect(idx6[:]))
+
+        hid = tile("hid", [P, O * PACK], BF16, tag="vs_plane")
+        nc.vector.tensor_tensor(
+            hid[:].rearrange("p (c i t) -> p c t i", i=4, t=PACK),
+            from_board[:].rearrange("p t (c i) -> p c t i", i=4),
+            from_b[:].rearrange("p t (c i) -> p c t i", i=4),
+            MAX,
+        )
+        hid_words = tile("hid_words", [P, O], U32)
+        hid_scales = tile("hid_scales", [P, O], U8)
+        nc.vector.quantize_mx(hid_words[:].bitcast(E4M3), hid_scales[:], hid[:])
+
+        for h in range(N // P):
+            p_bank = psum.tile([P, O], F32, name=f"p_bank{h}", tag=f"bank{h}")
+            cols = slice(h * P, (h + 1) * P)
+            nc.tensor.matmul_mx(
+                p_bank[:], lhsT=vw_picked[:, cols].bitcast(E2M1), lhsT_scale=vs_picked[:, cols],
+                rhs=hid_words[:].bitcast(E4M3), rhs_scale=hid_scales[:], start=True, stop=True,
+            )
+            p = tile(f"p{h}", [P, O], F32)
+            if h == 0:
+                nc.scalar.copy(p[:], p_bank[:])
+                nc.scalar.activation(pages[h][:].indirect(idx7[:]), p[:], COPY)
+                nc.scalar.dma_start(out[cols, :], pages[h][:])
+            else:
+                nc.vector.tensor_copy(p[:], p_bank[:])
+                nc.vector.tensor_copy(pages[h][:].indirect(idx7[:]), p[:])
+                nc.sync.dma_start(out[cols, :], pages[h][:])

@@ -116,9 +116,8 @@ def tile_list_leadseats_twow_store_scattered_kernel(
                 rhs=xw_picked[:].bitcast(E5M2), rhs_scale=xs_picked[:], start=True, stop=True,
             )
 
-        pages = [tile(f"page{h}", [P, E], F32, tag=tag) for h, tag in enumerate(("w2w_dealt", "ww_dealt"))]
-        for page in pages:
-            nc.gpsimd.memset(page[:], 0.0)
+        pages = [tile("page0", [P, E], F32, tag="ww")]
+        nc.vector.memset(pages[0][:], 0.0)
 
         a = [tile(f"a{t}", [P, J], F32) for t in range(PACK)]
         b = [tile(f"b{t}", [P, J], F32) for t in range(PACK)]
@@ -134,7 +133,9 @@ def tile_list_leadseats_twow_store_scattered_kernel(
 
         for t in range(PACK):
             nc.scalar.copy(b[t][:], b_bank[t][:])
-        for t in range(PACK):
+        nc.scalar.copy(a[0][:], a_bank[0][:])
+        seat(0)
+        for t in range(1, PACK):
             nc.vector.tensor_copy(a[t][:], a_bank[t][:])
             seat(t)
         for t in (0, 1):
@@ -161,6 +162,9 @@ def tile_list_leadseats_twow_store_scattered_kernel(
         hid_words = tile("hid_words", [P, O], U32)
         hid_scales = tile("hid_scales", [P, O], U8)
         nc.vector.quantize_mx(hid_words[:].bitcast(E4M3), hid_scales[:], hid[:])
+
+        pages.append(tile("page1", [P, E], F32, tag="vs_plane"))
+        nc.vector.memset(pages[1][:], 0.0)
 
         for h in range(N // P):
             p_bank = psum.tile([P, O], F32, name=f"p_bank{h}", tag=f"bank{h}")

from contextlib import ExitStack

import concourse.mybir as mybir

K, T, J, R, C, I, O, N, S, E = 512, 1024, 256, 512, 512, 128, 128, 256, 1024, 1024
FLOPS = 2 * (2 * K * R * J + R * N * O)

F32 = mybir.dt.float32
BF16 = mybir.dt.bfloat16
I32 = mybir.dt.int32
U32 = mybir.dt.uint32
U16 = mybir.dt.uint16
U8 = mybir.dt.uint8
E4M3 = mybir.dt.float8_e4m3fn_x4
E5M2 = mybir.dt.float8_e5m2_x4
E2M1 = mybir.dt.float4_e2m1fn_x4
COPY = mybir.ActivationFunctionType.Copy
MAX = mybir.AluOpType.max

P = 128
PACK = 4
QUADS = 4


def tile_list_leadseats_twow_store_scattered_kernel(
    tc, xt_words, xt_scales, w_words, w_scales, w2_words, w2_scales, vs_words, vs_scales,
    offs, offs2, offs3, offs4, offs5, offs6, offs7, out,
):
    nc = tc.nc
    with ExitStack() as ctx:
        lists = ctx.enter_context(tc.tile_pool(name="lists", bufs=1))
        sb = ctx.enter_context(tc.tile_pool(name="sb", bufs=1))
        psum = ctx.enter_context(tc.psum_pool(name="psum", bufs=1))

        def tile(name, shape, dtype, tag=""):
            return sb.tile(shape, dtype, name=name, tag=tag or name, align_bytes=64)

        def load_list(name, src):
            held = lists.tile([P, src.shape[1]], U16, name=name)
            nc.sync.dma_start(held[:], src)
            return held

        def zero_bytes(plane):
            nc.vector.memset(plane[:].bitcast(I32), 0)

        def load_scale_rows(plane, scales):
            rows = scales[0].bitcast(I32)
            for q in range(QUADS):
                nc.sync.dma_start(plane[:].bitcast(I32)[32 * q : 32 * q + 4, :], rows[4 * q : 4 * q + 4, :])

        def stage_scale_rows(name, scales, queue):
            staged = tile(name, [4, QUADS, R // 4], I32)
            queue.dma_start(staged[:], scales[0].bitcast(I32).rearrange("(q r) c -> r q c", r=4))
            return staged

        def deal_scale_rows(name, staged, plane):
            for q in range(QUADS):
                nc.vector.tensor_copy(plane[:].bitcast(I32)[32 * q : 32 * q + 4, :], staged[:, q, :])
            dealt = tile(name, [P, PACK, P], U8)
            nc.vector.tensor_copy(dealt[:].rearrange("p t m -> p m t"), plane[:].rearrange("p (m t) -> p m t", t=PACK))
            return dealt

        xs_plane = tile("xs_plane", [P, T], U8)
        ws_plane = tile("ws_plane", [P, R], U8)
        w2s_plane = tile("w2s_plane", [P, R], U8)
        vs_plane = tile("vs_plane", [P, S], U8)
        for plane in (xs_plane, w2s_plane, ws_plane, vs_plane):
            zero_bytes(plane)

        idx = load_list("idx", offs)
        w2s_staged = stage_scale_rows("w2s_staged", w2_scales, nc.scalar)
        w2w = tile("w2w", [P, R], I32)
        nc.sync.dma_start(w2w[:], w2_words[0].rearrange("p c t -> p (c t)").bitcast(I32))
        xw = tile("xw", [P, T], I32)
        nc.scalar.dma_start(xw[:], xt_words[0].rearrange("p c t -> p (c t)").bitcast(I32))
        load_scale_rows(xs_plane, xt_scales)
        ws_staged = stage_scale_rows("ws_staged", w_scales, nc.sync)
        ww = tile("ww", [P, R], U16)
        nc.sync.dma_start(ww[:].bitcast(I32), w_words[0].bitcast(I32))
        idx2 = load_list("idx2", offs2)
        idx3 = load_list("idx3", offs3)
        idx6 = load_list("idx6", offs6)
        vw = tile("vw", [P, S], U16)
        nc.sync.dma_start(vw[:].bitcast(I32), vs_words[0].bitcast(I32))
        idx5 = load_list("idx5", offs5)
        idx4 = load_list("idx4", offs4)
        load_scale_rows(vs_plane, vs_scales)
        idx7 = load_list("idx7", offs7)

        boards = [tile(f"board{t}", [P, C], F32) for t in range(PACK)]
        for board in boards:
            nc.vector.memset(board[:], 0.0)

        w2s_dealt = deal_scale_rows("w2s_dealt", w2s_staged, w2s_plane)
        w2w_dealt = tile("w2w_dealt", [P, PACK, P], U32)
        nc.scalar.copy(w2w_dealt[:].rearrange("p t m -> p m t"), w2w[:].bitcast(U32).rearrange("p (m t) -> p m t", t=PACK))
        xs_picked = tile("xs_picked", [P, J], U8)
        nc.vector.tensor_copy(xs_picked[:], xs_plane[:].indirect(idx[:]))
        xw_picked = tile("xw_picked", [P, J], U32, tag="xs_plane")
        nc.vector.tensor_copy(xw_picked[:], xw[:].bitcast(U32).indirect(idx[:]))
        ws_dealt = deal_scale_rows("ws_dealt", ws_staged, ws_plane)
        ww_dealt = tile("ww_dealt", [P, PACK, P], U16)
        nc.vector.tensor_copy(ww_dealt[:].rearrange("p t m -> p m t"), ww[:].rearrange("p (m t) -> p m t", t=PACK))

        a_bank, b_bank = [], []
        for t in range(PACK):
            b_bank.append(psum.tile([P, J], F32, name=f"b_bank{t}", tag=f"bank{t}"))
            nc.tensor.matmul_mx(
                b_bank[t][:], lhsT=w2w_dealt[:, t, :].bitcast(E4M3), lhsT_scale=w2s_dealt[:, t, :],
                rhs=xw_picked[:].bitcast(E5M2), rhs_scale=xs_picked[:], start=True, stop=True,
            )
        for t in range(PACK):
            a_bank.append(psum.tile([P, J], F32, name=f"a_bank{t}", tag=f"bank{PACK + t}"))
            nc.tensor.matmul_mx(
                a_bank[t][:], lhsT=ww_dealt[:, t, :].bitcast(E2M1), lhsT_scale=ws_dealt[:, t, :],
                rhs=xw_picked[:].bitcast(E5M2), rhs_scale=xs_picked[:], start=True, stop=True,
            )

        pages = [tile("page0", [P, E], F32, tag="ww")]
        nc.vector.memset(pages[0][:], 0.0)

        a = [tile(f"a{t}", [P, J], F32) for t in range(PACK)]
        b = [tile(f"b{t}", [P, J], F32) for t in range(PACK)]
        seats = [tile(f"seats{t}", [P, I], F32) for t in range(PACK)]
        from_board = tile("from_board", [P, PACK, O], F32)
        from_b = tile("from_b", [P, PACK, O], F32)

        def seat(t):
            nc.scalar.activation(seats[t][:], a[t][:].indirect(idx2[:]), COPY, scale=b[t][:, 0:1])

        def rival(t):
            nc.scalar.activation(from_b[:, t, :], b[t][:].indirect(idx5[:]), COPY, scale=a[t][:, 0:1])

        for t in range(PACK):
            nc.scalar.copy(b[t][:], b_bank[t][:])
        nc.scalar.copy(a[0][:], a_bank[0][:])
        seat(0)
        for t in range(1, PACK):
            nc.vector.tensor_copy(a[t][:], a_bank[t][:])
            seat(t)
        for t in (0, 1):
            nc.vector.tensor_copy(boards[t][:].indirect(idx3[:]), seats[t][:])
        for t in (2, 3):
            nc.scalar.activation(boards[t][:].indirect(idx3[:]), seats[t][:], COPY)
        vw_picked = tile("vw_picked", [P, N], U16)
        nc.vector.tensor_copy(vw_picked[:], vw[:].indirect(idx6[:]))
        for t in range(PACK):
            rival(t)
        for t in (0, 1, 2):
            nc.vector.tensor_copy(from_board[:, t, :], boards[t][:].indirect(idx4[:]))
        nc.scalar.activation(from_board[:, 3, :], boards[3][:].indirect(idx4[:]), COPY)
        vs_picked = tile("vs_picked", [P, N], U8)
        nc.vector.tensor_copy(vs_picked[:], vs_plane[:].indirect(idx6[:]))

        hid = tile("hid", [P, O * PACK], BF16, tag="vs_plane")
        nc.vector.tensor_tensor(
            hid[:].rearrange("p (c i t) -> p c t i", i=4, t=PACK),
            from_board[:].rearrange("p t (c i) -> p c t i", i=4),
            from_b[:].rearrange("p t (c i) -> p c t i", i=4),
            MAX,
        )
        hid_words = tile("hid_words", [P, O], U32)
        hid_scales = tile("hid_scales", [P, O], U8)
        nc.vector.quantize_mx(hid_words[:].bitcast(E4M3), hid_scales[:], hid[:])

        pages.append(tile("page1", [P, E], F32, tag="vs_plane"))
        nc.vector.memset(pages[1][:], 0.0)

        for h in range(N // P):
            p_bank = psum.tile([P, O], F32, name=f"p_bank{h}", tag=f"bank{h}")
            cols = slice(h * P, (h + 1) * P)
            nc.tensor.matmul_mx(
                p_bank[:], lhsT=vw_picked[:, cols].bitcast(E2M1), lhsT_scale=vs_picked[:, cols],
                rhs=hid_words[:].bitcast(E4M3), rhs_scale=hid_scales[:], start=True, stop=True,
            )
            p = tile(f"p{h}", [P, O], F32)
            if h == 0:
                nc.scalar.copy(p[:], p_bank[:])
                nc.scalar.activation(pages[h][:].indirect(idx7[:]), p[:], COPY)
                nc.scalar.dma_start(out[cols, :], pages[h][:])
            else:
                nc.vector.tensor_copy(p[:], p_bank[:])
                nc.vector.tensor_copy(pages[h][:].indirect(idx7[:]), p[:])
                nc.sync.dma_start(out[cols, :], pages[h][:])
